import numpy as np
import ml_dtypes


def mxq(x, axis, fmt="e4m3"):
    dtype, down = {"e4m3": (ml_dtypes.float8_e4m3fn, 7), "e5m2": (ml_dtypes.float8_e5m2, 14)}[fmt]
    v = np.moveaxis(np.asarray(x, np.float32).astype(ml_dtypes.bfloat16).astype(np.float64), axis, -1)
    blocks = v.reshape(v.shape[:-1] + (-1, 32))
    amax = np.abs(blocks).max(-1, keepdims=True)
    byte = np.maximum(np.where(amax > 0, np.frexp(amax)[1] - 1 + 127, 0) - down, 1)
    scale = np.exp2(byte - 127.0)
    codes = (blocks / scale).astype(np.float32).astype(dtype).astype(np.float64)
    return np.moveaxis((codes * scale).reshape(v.shape), -1, axis)


WIDE = False


def mx_kscale(k):
    if not WIDE:
        return np.ones(k)
    levels = np.array([10, -10, 5, -5, 0])
    if k % 512:
        return np.exp2(np.random.permutation(np.resize(levels, k // 32))).repeat(32)
    a = np.empty((k // 512, 16))
    for p in range(k // 512):
        a[p, :8] = np.random.permutation(np.resize(levels, 8))
        for g in range(8):
            far = levels[np.abs(levels - a[p, g]) >= 10]
            a[p, g + 8] = far[np.random.randint(len(far))]
    return np.exp2(a.ravel()).repeat(32)


def f64(x):
    return np.asarray(x).astype(np.float64)


def striped(idx):
    return np.tile(idx.reshape(-1, 16).T, (8, 1)).astype(np.uint16)


def unstriped(offs):
    return offs[:16].T.reshape(-1).astype(np.int64)


E2M1 = np.array([0.0, 0.5, 1.0, 1.5, 2.0, 3.0, 4.0, 6.0, -0.0, -0.5, -1.0, -1.5, -2.0, -3.0, -4.0, -6.0])


def pack_weight(w, fmt):
    k, n = w.shape
    w = f64(np.asarray(w, np.float32).astype(ml_dtypes.bfloat16)).reshape(k // 32, 32, n)
    amax = np.abs(w).max(1)
    if fmt == "e4m3":
        byte = np.frexp(amax)[1] - 1 + 127 - 7
    else:
        mant, ex = np.frexp(amax / 6.0)
        byte = np.where(mant > 0.5, ex, ex - 1) + 127
    byte = np.clip(np.where(amax > 0, byte, 1), 1, 254)
    scaled = (w * np.exp2(127.0 - byte)[:, None, :]).reshape(k, n).astype(np.float32)
    by_word = np.ascontiguousarray(scaled.reshape(k // 512, 128, 4, n).transpose(0, 1, 3, 2))
    if fmt == "e4m3":
        words = by_word.astype(ml_dtypes.float8_e4m3fn).view(np.uint8)
    else:
        c = by_word.astype(ml_dtypes.float4_e2m1fn).view(np.uint8) & 0xF
        words = (c[..., 0::2] | (c[..., 1::2] << 4)).reshape(k // 512, 128, 2 * n)
    return np.ascontiguousarray(words), np.ascontiguousarray(byte.astype(np.uint8).reshape(k // 512, 16, n))


def unpack_weight(words, scales, fmt):
    g, _, n = scales.shape
    words = np.ascontiguousarray(words).reshape(g, 128, n, -1)
    if fmt == "e4m3":
        vals = words.view(ml_dtypes.float8_e4m3fn).astype(np.float64)
    else:
        nib = np.empty((g, 128, n, 4), np.uint8)
        nib[..., 0::2] = words & 0xF
        nib[..., 1::2] = words >> 4
        vals = E2M1[nib]
    vals = vals * np.repeat(np.exp2(scales.astype(np.float64) - 127.0), 8, axis=1)[..., None]
    return vals.transpose(0, 1, 3, 2).reshape(g * 512, n)


def gelu(v):
    return 0.5 * v * (1.0 + np.tanh(np.sqrt(2.0 / np.pi) * (v + 0.044715 * v**3)))


def often(T, S):
    return np.random.permutation(T)[(T * np.random.uniform(0, 1, S) ** 4).astype(np.int64)]


K, M, H, N, T, S, P = 1024, 512, 1024, 512, 2048, 1024, 512

def setup_inputs():
    n = np.random.standard_normal
    s1 = mx_kscale(K)[:, None]
    s2 = mx_kscale(M)[:, None]
    u = mx_kscale(H)[:, None]
    d = {}
    d["tab_words"], d["tab_scales"] = pack_weight(n((K, T)) * s1, "e4m3")
    d["tab2_words"], d["tab2_scales"] = pack_weight(n((M, T)) * s2, "e4m3")
    d["tab3_words"], d["tab3_scales"] = pack_weight(n((M, T)) * s2, "e4m3")
    d["offs"] = striped(np.random.permutation(T)[:S])
    d["offs2"] = striped(np.random.permutation(T)[:S])
    d["offs3"] = striped(np.random.permutation(T)[:S])
    d["pos1"] = striped(np.random.permutation(S)[:P])
    d["pos2"] = striped(often(S, P))
    d["pos3"] = striped(often(S, P))
    d["w1"] = (n((K, H)) / K ** 0.5 / s1 * u.T).astype(np.float32)
    d["w2_words"], d["w2_scales"] = pack_weight(n((M, H)) / M ** 0.5 / s2, "e2m1")
    d["bias2"] = (0.6 * n(H)).astype(np.float32)
    d["w3"] = (n((M, H)) / M ** 0.5 / s2 * u.T).astype(np.float32)
    d["w4_words"], d["w4_scales"] = pack_weight(n((H, N)) / H ** 0.5 / u, "e4m3")
    d["w5"] = (n((H, N)) / H ** 0.5 / u).astype(np.float32)
    d["bias5"] = (0.8 * n(N)).astype(np.float32)
    return d

def reference(tab_words, tab_scales, tab2_words, tab2_scales, tab3_words, tab3_scales, offs, offs2, offs3,
              pos1, pos2, pos3, w1, w2_words, w2_scales, bias2, w3, w4_words, w4_scales, w5, bias5):
    v = unpack_weight(tab_words, tab_scales, "e4m3")[:, unstriped(offs)]
    v2 = unpack_weight(tab2_words, tab2_scales, "e4m3")[:, unstriped(offs2)]
    v3 = unpack_weight(tab3_words, tab3_scales, "e4m3")[:, unstriped(offs3)]
    a = mxq(f64(w1), 0, "e4m3").T @ v
    b = (unpack_weight(w2_words, w2_scales, "e2m1").T @ v2) + f64(bias2)[:, None]
    d = mxq(f64(w3), 0, "e4m3").T @ v3
    z = a[:, unstriped(pos1)] * b[:, unstriped(pos2)] + d[:, unstriped(pos3)]
    zq = mxq(z, 0, "e4m3")
    y1 = unpack_weight(w4_words, w4_scales, "e4m3").T @ zq
    y2 = (mxq(f64(w5), 0, "e4m3").T @ zq) + f64(bias5)[:, None]
    return y1 / (1.0 + np.abs(y2))

@@ -1,0 +1,274 @@
+from contextlib import ExitStack
+
+import concourse.mybir as mybir
+
+K, M, H, N, T, S, J = 1024, 512, 1024, 512, 2048, 1024, 512
+FLOPS = 2 * (K * H * S + 2 * M * H * S + 2 * H * N * J)
+
+F32 = mybir.dt.float32
+BF16 = mybir.dt.bfloat16
+I32 = mybir.dt.int32
+U32 = mybir.dt.uint32
+U16 = mybir.dt.uint16
+U8 = mybir.dt.uint8
+FP8X4 = mybir.dt.float8_e4m3fn_x4
+FP4X4 = mybir.dt.float4_e2m1fn_x4
+ACT = mybir.ActivationFunctionType
+ALU = mybir.AluOpType
+
+P = 128
+PACK = 4
+PASS = P * PACK
+BANK = 512
+SLICES = (128, 128, 128, 128)
+RB = 3
+
+
+def tile_list_pump_inspection_join_kernel(
+    tc, tab_words, tab_scales, tab2_words, tab2_scales, tab3_words, tab3_scales, offs, offs2, offs3,
+    pos1, pos2, pos3, w1, w2_words, w2_scales, bias2, w3, w4_words, w4_scales, w5, bias5, out,
+):
+    nc = tc.nc
+    with ExitStack() as ctx:
+        lists = ctx.enter_context(tc.tile_pool(name="lists", bufs=1))
+        sb = ctx.enter_context(tc.tile_pool(name="sb", bufs=1))
+        psum = ctx.enter_context(tc.psum_pool(name="psum", bufs=8))
+
+        def load_list(src, name):
+            t = lists.tile(list(src.shape), U16, name=name)
+            nc.sync.dma_start(t[:], src)
+            return t
+
+        def plane_tile(width, name, engine):
+            t = sb.tile([P, width], U8, name=name, align_bytes=64)
+            engine.memset(t[:].bitcast(I32), 0)
+            return t
+
+        def load_planes(t, scales, queue):
+            rows = 4 * scales.shape[0]
+            for q in range(4):
+                queue.dma_start(
+                    t[32 * q : 32 * q + rows, :].bitcast(I32), scales[:, 4 * q : 4 * q + 4, :].bitcast(I32)
+                )
+
+        def load_words(words, name):
+            t = sb.tile([P, T], U32, name=name, tag="big", bufs=6, align_bytes=64)
+            nc.sync.dma_start(t[:].bitcast(I32), words.rearrange("p t i -> p (t i)").bitcast(I32))
+            return t
+
+        def load_weight(w, a, g, name):
+            t = sb.tile([P, PACK, PASS], F32, name=name, tag="big", bufs=6, align_bytes=64)
+            src = w[a * PASS : (a + 1) * PASS, g * PASS : (g + 1) * PASS]
+            nc.sync.dma_start(t[:], src.rearrange("(p j) c -> p j c", j=PACK))
+            return t
+
+        s2 = plane_tile(T, "s2", nc.gpsimd)
+        w2s = plane_tile(H, "w2s", nc.vector)
+        s1 = plane_tile(T, "s1", nc.gpsimd)
+        s3 = plane_tile(T, "s3", nc.vector)
+        w4s = plane_tile(N, "w4s", nc.vector)
+        raw1, raw3, raw5, t1 = {}, {}, {}, {}
+        l2 = load_list(offs2, "l2")
+        load_planes(s2, tab2_scales, nc.sync)
+        t2 = load_words(tab2_words[0], "t2")
+        w2w = sb.tile([P, 2 * H], U8, name="w2w", align_bytes=64)
+        nc.sync.dma_start(w2w[:].bitcast(I32), w2_words[0].bitcast(I32))
+        raw1[0, 0] = load_weight(w1, 0, 0, "raw100")
+        raw1[1, 0] = load_weight(w1, 1, 0, "raw110")
+        load_planes(w2s, w2_scales, nc.sync)
+        t1[0] = load_words(tab_words[0], "t10")
+        l1 = load_list(offs, "l1")
+        load_planes(s1, tab_scales, nc.sync)
+        b2 = sb.tile([P, 2 * PACK], F32, name="b2")
+        nc.sync.dma_start(
+            b2[:].rearrange("p (g t) -> p g t", t=PACK), bias2.rearrange("(g p t) -> p g t", p=P, t=PACK)
+        )
+        t1[1] = load_words(tab_words[1], "t11")
+        load_planes(s3, tab3_scales, nc.sync)
+        raw3[0] = load_weight(w3, 0, 0, "raw30")
+        l3 = load_list(offs3, "l3")
+        p2 = load_list(pos2, "p2")
+        raw1[0, 1] = load_weight(w1, 0, 1, "raw101")
+        t3 = load_words(tab3_words[0], "t3")
+        raw1[1, 1] = load_weight(w1, 1, 1, "raw111")
+        load_planes(w4s, w4_scales, nc.sync)
+        raw3[1] = load_weight(w3, 0, 1, "raw31")
+        p1 = load_list(pos1, "p1")
+        p3 = load_list(pos3, "p3")
+        raw5[0] = load_weight(w5, 0, 0, "raw50")
+        raw5[1] = load_weight(w5, 1, 0, "raw51")
+        w4w = sb.tile([P, 2, N], U32, name="w4w", align_bytes=64)
+        nc.sync.dma_start(w4w[:].bitcast(I32), w4_words.rearrange("g p c i -> p g (c i)").bitcast(I32))
+        b5 = sb.tile([P, N // P], F32, name="b5")
+        with nc.allow_non_contiguous_dma(reason="one bias value to a partition"):
+            nc.sync.dma_start(b5[:], bias5.rearrange("(c p) -> p c", p=P))
+
+        def gather(window, offsets, dtype, name):
+            t = sb.tile([P, S], dtype, name=name, align_bytes=64)
+            nc.vector.tensor_copy(t[:], window[:].indirect(offsets[:]))
+            return t
+
+        def deal(raw):
+            t = sb.tile([P, PACK * PASS], BF16, name="rounded", tag="rounded", bufs=RB, align_bytes=64)
+            nc.scalar.copy(
+                t[:].rearrange("p (t m u e) -> p m u t e", t=PACK, u=2, e=2),
+                raw[:].rearrange("p (u e) (m t) -> p m u t e", e=2, t=PACK),
+            )
+            return t
+
+        def weave(raw, tag, bufs, copy):
+            width = raw.shape[2]
+            t = sb.tile([P, PACK * width], BF16, name=tag, tag=tag, bufs=bufs, align_bytes=64)
+            copy(
+                t[:].rearrange("p (c i j) -> p c j i", i=4, j=PACK),
+                raw.rearrange("p j (c i) -> p c j i", i=4),
+            )
+            return t
+
+        def quantise(rounded, name):
+            width = rounded.shape[1] // PACK
+            codes = sb.tile([P, width], U32, name=name + "c", align_bytes=64)
+            plane = sb.tile([P, width], U8, name=name + "s", align_bytes=64)
+            nc.vector.quantize_mx(out=codes[:].bitcast(FP8X4), scales=plane[:], in_=rounded[:])
+            return codes, plane
+
+        def project(passes, bias):
+            win = sb.tile([P, S], F32, name="win", tag="win", bufs=16)
+            for h in range(S // BANK):
+                cols = slice(h * BANK, (h + 1) * BANK)
+                bank = psum.tile([P, BANK], F32, name="bank", tag="bank")
+                for a, (wc, ws, vc, vs) in enumerate(passes):
+                    nc.tensor.matmul_mx(
+                        out=bank[:], lhsT=wc, lhsT_scale=ws, rhs=vc[:, cols].bitcast(FP8X4), rhs_scale=vs[:, cols],
+                        start=(a == 0), stop=(a == len(passes) - 1),
+                    )
+                if bias is None:
+                    nc.scalar.copy(win[:, cols], bank[:])
+                else:
+                    nc.scalar.activation(win[:, cols], bank[:], ACT.Identity, bias=bias)
+            return win
+
+        def fuel(g):
+            picks = []
+            for t in range(PACK):
+                c0 = g * PASS + t * P
+                win = project(
+                    [(w2wp[:, 2 * c0 : 2 * (c0 + P)].bitcast(FP4X4), w2sp[:, c0 : c0 + P], g2w, g2s)],
+                    b2[:, PACK * g + t : PACK * g + t + 1],
+                )
+                pick = sb.tile([P, J], F32, name="pick", tag="pick", bufs=8)
+                nc.vector.tensor_copy(pick[:], win[:].indirect(p2[:]))
+                picks.append(pick)
+            return picks
+
+        def pumps(g, picks):
+            prods = []
+            for t in range(PACK):
+                cols = slice(t * P, (t + 1) * P)
+                win = project(
+                    [
+                        (q1[a, g][0][:, cols].bitcast(FP8X4), q1[a, g][1][:, cols], g1w[a], g1s[4 * a :, :])
+                        for a in range(2)
+                    ],
+                    None,
+                )
+                ab = sb.tile([P, J], F32, name="prod", tag="prod", bufs=8)
+                nc.vector.tensor_tensor(ab[:], win[:].indirect(p1[:]), picks[t][:], ALU.mult)
+                prods.append(ab)
+            return prods
+
+        def cans(g):
+            wins = []
+            for t in range(PACK):
+                cols = slice(t * P, (t + 1) * P)
+                wins.append(project([(q3[g][0][:, cols].bitcast(FP8X4), q3[g][1][:, cols], g3w, g3s)], None))
+            return wins
+
+        def join(z, wins, prods, j0, width):
+            for t in range(PACK):
+                nc.vector.tensor_tensor(
+                    z[:, t, :], wins[t][:].indirect(p3[:, j0 // 16 : (j0 + width) // 16]),
+                    prods[t][:, j0 : j0 + width], ALU.add,
+                )
+
+        q1, q3, q5, g1w = {}, {}, {}, {}
+        g2s = gather(s2, l2, U8, "g2s")
+        w2wp = sb.tile([P, 2 * H], U8, name="w2wp", align_bytes=64)
+        nc.scalar.copy(
+            w2wp[:].bitcast(U16).rearrange("p (g t m) -> p g t m", g=2, t=PACK),
+            w2w[:].bitcast(U16).rearrange("p (g m t) -> p g t m", g=2, t=PACK),
+        )
+        g2w = gather(t2, l2, U32, "g2w")
+        w2sp = sb.tile([P, H], U8, name="w2sp", align_bytes=64)
+        nc.vector.tensor_copy(
+            w2sp[:].rearrange("p (g t m) -> p g t m", g=2, t=PACK), w2s[:].rearrange("p (g m t) -> p g t m", g=2, t=PACK)
+        )
+        q1[0, 0] = quantise(deal(raw1[0, 0]), "q100")
+        q1[1, 0] = quantise(deal(raw1[1, 0]), "q110")
+        q3[0] = quantise(deal(raw3[0]), "q30")
+        q1[0, 1] = quantise(deal(raw1[0, 1]), "q101")
+        q1[1, 1] = quantise(deal(raw1[1, 1]), "q111")
+        q3[1] = quantise(deal(raw3[1]), "q31")
+        g1s = gather(s1, l1, U8, "g1s")
+        g1w[0] = gather(t1[0], l1, U32, "g1w0")
+        g1w[1] = gather(t1[1], l1, U32, "g1w1")
+        g3s = gather(s3, l3, U8, "g3s")
+        g3w = gather(t3, l3, U32, "g3w")
+        picks0 = fuel(0)
+        picks1 = fuel(1)
+        q5[0] = quantise(weave(raw5[0][:], "rounded", RB, nc.scalar.copy), "q50")
+        q5[1] = quantise(weave(raw5[1][:], "rounded", RB, nc.vector.tensor_copy), "q51")
+        prods0 = pumps(0, picks0)
+        wins0 = cans(0)
+        z0 = sb.tile([P, PACK, J], F32, name="z0", tag="z0")
+        join(z0, wins0, prods0, 0, J)
+        prods1 = pumps(1, picks1)
+        wins1 = cans(1)
+        zq0 = quantise(weave(z0[:], "rounded", RB, nc.scalar.copy), "zq0")
+        zfirst = sb.tile([P, PACK, SLICES[0]], F32, name="zfirst")
+        zrest = sb.tile([P, PACK * (J - SLICES[0])], F32, name="zrest", tag="z0")
+
+        j0 = 0
+        for s, width in enumerate(SLICES):
+            jcols = slice(j0, j0 + width)
+            per_bank = BANK // width
+            nbanks = (N // P) // per_bank
+            if s == 0:
+                z = zfirst[:]
+            else:
+                z = zrest[:, PACK * (j0 - SLICES[0]) : PACK * (j0 - SLICES[0] + width)].rearrange("p (t j) -> p t j", t=PACK)
+            join(z, wins1, prods1, j0, width)
+            last = s == len(SLICES) - 1
+            zq1 = quantise(weave(z, "zround", 2, nc.vector.tensor_copy if last else nc.scalar.copy), "zq1%d" % s)
+            y1 = [psum.tile([P, BANK], F32, name="bank", tag="bank") for b in range(nbanks)]
+            y2 = [psum.tile([P, BANK], F32, name="bank", tag="bank") for b in range(nbanks)]
+            for g, (zc, zs) in enumerate(((zq0[0][:, jcols], zq0[1][:, jcols]), (zq1[0][:], zq1[1][:]))):
+                for banks, wc, ws in (
+                    (y2, q5[g][0][:], q5[g][1][:]),
+                    (y1, w4w[:, g, :], w4s[4 * g :, :]),
+                ):
+                    for c in range(N // P):
+                        place = c % per_bank
+                        nc.tensor.matmul_mx(
+                            out=banks[c // per_bank][:, place * width : (place + 1) * width],
+                            lhsT=wc[:, c * P : (c + 1) * P].bitcast(FP8X4), lhsT_scale=ws[:, c * P : (c + 1) * P],
+                            rhs=zc.bitcast(FP8X4), rhs_scale=zs,
+                            start=(g == 0 and place == 0), stop=(g == 1 and place == per_bank - 1),
+                        )
+            for b in range(nbanks):
+                size = sb.tile([P, BANK], F32, name="pick", tag="pick", bufs=8)
+                for place in range(per_bank):
+                    c = b * per_bank + place
+                    cols = slice(place * width, (place + 1) * width)
+                    nc.scalar.activation(size[:, cols], y2[b][:, cols], ACT.Abs, bias=b5[:, c : c + 1])
+                root = sb.tile([P, BANK], F32, name="pick", tag="pick", bufs=8)
+                nc.scalar.activation(root[:], size[:], ACT.Abs_reciprocal_sqrt, bias=1.0)
+                inv = sb.tile([P, BANK], F32, name="pick", tag="pick", bufs=8)
+                nc.vector.tensor_tensor(inv[:], y1[b][:], root[:], ALU.mult)
+                res = sb.tile([P, BANK], F32, name="pick", tag="pick", bufs=8)
+                nc.vector.tensor_tensor(res[:], inv[:], root[:], ALU.mult)
+                rows = out[b * per_bank * P : (b + 1) * per_bank * P, jcols]
+                nc.sync.dma_start(
+                    rows.rearrange("(c p) j -> p c j", p=P), res[:].rearrange("p (c j) -> p c j", j=width)
+                )
+            j0 = j0 + width

@@ -39,17 +39,22 @@ def tile_list_pump_inspection_join_kernel(
             nc.sync.dma_start(t[:], src)
             return t
 
-        def plane_tile(width, name, engine):
+        def plane_tile(width, name, *engines):
             t = sb.tile([P, width], U8, name=name, align_bytes=64)
-            engine.memset(t[:].bitcast(I32), 0)
+            share = width // len(engines)
+            for n, engine in enumerate(engines):
+                engine.memset(t[:, n * share : (n + 1) * share].bitcast(I32), 0)
             return t
 
         def load_planes(t, scales, queue):
             rows = 4 * scales.shape[0]
             for q in range(4):
-                queue.dma_start(
-                    t[32 * q : 32 * q + rows, :].bitcast(I32), scales[:, 4 * q : 4 * q + 4, :].bitcast(I32)
-                )
+                if rows == 4:
+                    queue.dma_start(t[q:P:32, :].bitcast(I32), scales[0, q:16:4, :].bitcast(I32))
+                else:
+                    queue.dma_start(
+                        t[32 * q : 32 * q + rows, :].bitcast(I32), scales[:, 4 * q : 4 * q + 4, :].bitcast(I32)
+                    )
 
         def load_words(words, name):
             t = sb.tile([P, T], U32, name=name, tag="big", bufs=6, align_bytes=64)
@@ -62,34 +67,34 @@ def tile_list_pump_inspection_join_kernel(
             nc.sync.dma_start(t[:], src.rearrange("(p j) c -> p j c", j=PACK))
             return t
 
-        s2 = plane_tile(T, "s2", nc.gpsimd)
-        w2s = plane_tile(H, "w2s", nc.vector)
-        s1 = plane_tile(T, "s1", nc.gpsimd)
-        s3 = plane_tile(T, "s3", nc.vector)
-        w4s = plane_tile(N, "w4s", nc.vector)
+        s2 = plane_tile(T, "s2", nc.gpsimd, nc.vector)
+        w2s = plane_tile(H, "w2s", nc.gpsimd)
+        s1 = plane_tile(T, "s1", nc.vector)
+        s3 = plane_tile(T, "s3", nc.gpsimd)
+        w4s = plane_tile(N, "w4s", nc.gpsimd)
         raw1, raw3, raw5, t1 = {}, {}, {}, {}
         l2 = load_list(offs2, "l2")
         load_planes(s2, tab2_scales, nc.sync)
-        t2 = load_words(tab2_words[0], "t2")
         w2w = sb.tile([P, 2 * H], U8, name="w2w", align_bytes=64)
         nc.sync.dma_start(w2w[:].bitcast(I32), w2_words[0].bitcast(I32))
-        raw1[0, 0] = load_weight(w1, 0, 0, "raw100")
-        raw1[1, 0] = load_weight(w1, 1, 0, "raw110")
-        load_planes(w2s, w2_scales, nc.sync)
-        t1[0] = load_words(tab_words[0], "t10")
         l1 = load_list(offs, "l1")
+        t2 = load_words(tab2_words[0], "t2")
+        load_planes(w2s, w2_scales, nc.sync)
+        raw1[0, 0] = load_weight(w1, 0, 0, "raw100")
         load_planes(s1, tab_scales, nc.sync)
+        t1[0] = load_words(tab_words[0], "t10")
         b2 = sb.tile([P, 2 * PACK], F32, name="b2")
         nc.sync.dma_start(
             b2[:].rearrange("p (g t) -> p g t", t=PACK), bias2.rearrange("(g p t) -> p g t", p=P, t=PACK)
         )
-        t1[1] = load_words(tab_words[1], "t11")
-        load_planes(s3, tab3_scales, nc.sync)
-        raw3[0] = load_weight(w3, 0, 0, "raw30")
         l3 = load_list(offs3, "l3")
+        load_planes(s3, tab3_scales, nc.sync)
+        t1[1] = load_words(tab_words[1], "t11")
         p2 = load_list(pos2, "p2")
-        raw1[0, 1] = load_weight(w1, 0, 1, "raw101")
+        raw1[1, 0] = load_weight(w1, 1, 0, "raw110")
+        raw3[0] = load_weight(w3, 0, 0, "raw30")
         t3 = load_words(tab3_words[0], "t3")
+        raw1[0, 1] = load_weight(w1, 0, 1, "raw101")
         raw1[1, 1] = load_weight(w1, 1, 1, "raw111")
         load_planes(w4s, w4_scales, nc.sync)
         raw3[1] = load_weight(w3, 0, 1, "raw31")
@@ -223,23 +228,18 @@ def tile_list_pump_inspection_join_kernel(
         z0 = sb.tile([P, PACK, J], F32, name="z0", tag="z0")
         join(z0, wins0, prods0, 0, J)
         prods1 = pumps(1, picks1)
-        wins1 = cans(1)
         zq0 = quantise(weave(z0[:], "rounded", RB, nc.scalar.copy), "zq0")
-        zfirst = sb.tile([P, PACK, SLICES[0]], F32, name="zfirst")
-        zrest = sb.tile([P, PACK * (J - SLICES[0])], F32, name="zrest", tag="z0")
+        wins1 = cans(1)
 
         j0 = 0
         for s, width in enumerate(SLICES):
             jcols = slice(j0, j0 + width)
             per_bank = BANK // width
             nbanks = (N // P) // per_bank
-            if s == 0:
-                z = zfirst[:]
-            else:
-                z = zrest[:, PACK * (j0 - SLICES[0]) : PACK * (j0 - SLICES[0] + width)].rearrange("p (t j) -> p t j", t=PACK)
+            ztile = sb.tile([P, PACK, width], F32, name="z1", tag="z1", bufs=2)
+            z = ztile[:]
             join(z, wins1, prods1, j0, width)
-            last = s == len(SLICES) - 1
-            zq1 = quantise(weave(z, "zround", 2, nc.vector.tensor_copy if last else nc.scalar.copy), "zq1%d" % s)
+            zq1 = quantise(weave(z, "zround", 2, nc.vector.tensor_copy if "ssvv"[s] == "v" else nc.scalar.copy), "zq1%d" % s)
             y1 = [psum.tile([P, BANK], F32, name="bank", tag="bank") for b in range(nbanks)]
             y2 = [psum.tile([P, BANK], F32, name="bank", tag="bank") for b in range(nbanks)]
             for g, (zc, zs) in enumerate(((zq0[0][:, jcols], zq0[1][:, jcols]), (zq1[0][:], zq1[1][:]))):
@@ -255,20 +255,28 @@ def tile_list_pump_inspection_join_kernel(
                             rhs=zc.bitcast(FP8X4), rhs_scale=zs,
                             start=(g == 0 and place == 0), stop=(g == 1 and place == per_bank - 1),
                         )
+            parts = 2 if s == len(SLICES) - 1 else 1
+            group = per_bank // parts
             for b in range(nbanks):
                 size = sb.tile([P, BANK], F32, name="pick", tag="pick", bufs=8)
-                for place in range(per_bank):
-                    c = b * per_bank + place
-                    cols = slice(place * width, (place + 1) * width)
-                    nc.scalar.activation(size[:, cols], y2[b][:, cols], ACT.Abs, bias=b5[:, c : c + 1])
                 root = sb.tile([P, BANK], F32, name="pick", tag="pick", bufs=8)
-                nc.scalar.activation(root[:], size[:], ACT.Abs_reciprocal_sqrt, bias=1.0)
-                inv = sb.tile([P, BANK], F32, name="pick", tag="pick", bufs=8)
-                nc.vector.tensor_tensor(inv[:], y1[b][:], root[:], ALU.mult)
+                half = sb.tile([P, BANK], F32, name="pick", tag="pick", bufs=8)
                 res = sb.tile([P, BANK], F32, name="pick", tag="pick", bufs=8)
-                nc.vector.tensor_tensor(res[:], inv[:], root[:], ALU.mult)
-                rows = out[b * per_bank * P : (b + 1) * per_bank * P, jcols]
-                nc.sync.dma_start(
-                    rows.rearrange("(c p) j -> p c j", p=P), res[:].rearrange("p (c j) -> p c j", j=width)
-                )
+                for part in range(parts):
+                    c0 = b * per_bank + part * group
+                    span = slice(part * group * width, (part + 1) * group * width)
+                    for c in range(c0, c0 + group):
+                        cols = slice((c % per_bank) * width, (c % per_bank + 1) * width)
+                        nc.scalar.activation(size[:, cols], y2[b][:, cols], ACT.Abs, bias=b5[:, c : c + 1])
+                    nc.scalar.activation(root[:, span], size[:, span], ACT.Abs_reciprocal_sqrt, bias=1.0)
+                    if "vvvv"[s] == "s":
+                        nc.scalar.activation(half[:, span], root[:, span], ACT.Square)
+                        nc.vector.tensor_tensor(res[:, span], y1[b][:, span], half[:, span], ALU.mult)
+                    else:
+                        nc.vector.tensor_tensor(half[:, span], y1[b][:, span], root[:, span], ALU.mult)
+                        nc.vector.tensor_tensor(res[:, span], half[:, span], root[:, span], ALU.mult)
+                    rows = out[c0 * P : (c0 + group) * P, jcols]
+                    nc.sync.dma_start(
+                        rows.rearrange("(c p) j -> p c j", p=P), res[:, span].rearrange("p (c j) -> p c j", j=width)
+                    )
             j0 = j0 + width

@@ -21,7 +21,7 @@ PACK = 4
 PASS = P * PACK
 BANK = 512
 SLICES = (128, 128, 128, 128)
-RB = 3
+RB = 4
 
 
 def tile_list_pump_inspection_join_kernel(
@@ -68,8 +68,8 @@ def tile_list_pump_inspection_join_kernel(
             return t
 
         s2 = plane_tile(T, "s2", nc.gpsimd, nc.vector)
-        w2s = plane_tile(H, "w2s", nc.gpsimd)
         s1 = plane_tile(T, "s1", nc.vector)
+        w2s = plane_tile(H, "w2s", nc.gpsimd)
         s3 = plane_tile(T, "s3", nc.gpsimd)
         w4s = plane_tile(N, "w4s", nc.gpsimd)
         raw1, raw3, raw5, t1 = {}, {}, {}, {}
@@ -79,29 +79,29 @@ def tile_list_pump_inspection_join_kernel(
         nc.sync.dma_start(w2w[:].bitcast(I32), w2_words[0].bitcast(I32))
         l1 = load_list(offs, "l1")
         t2 = load_words(tab2_words[0], "t2")
-        load_planes(w2s, w2_scales, nc.sync)
-        raw1[0, 0] = load_weight(w1, 0, 0, "raw100")
+        l3 = load_list(offs3, "l3")
         load_planes(s1, tab_scales, nc.sync)
-        t1[0] = load_words(tab_words[0], "t10")
+        raw1[0, 0] = load_weight(w1, 0, 0, "raw100")
+        load_planes(w2s, w2_scales, nc.sync)
+        raw1[1, 0] = load_weight(w1, 1, 0, "raw110")
         b2 = sb.tile([P, 2 * PACK], F32, name="b2")
         nc.sync.dma_start(
             b2[:].rearrange("p (g t) -> p g t", t=PACK), bias2.rearrange("(g p t) -> p g t", p=P, t=PACK)
         )
-        l3 = load_list(offs3, "l3")
         load_planes(s3, tab3_scales, nc.sync)
+        t1[0] = load_words(tab_words[0], "t10")
         t1[1] = load_words(tab_words[1], "t11")
-        p2 = load_list(pos2, "p2")
-        raw1[1, 0] = load_weight(w1, 1, 0, "raw110")
-        raw3[0] = load_weight(w3, 0, 0, "raw30")
         t3 = load_words(tab3_words[0], "t3")
+        p2 = load_list(pos2, "p2")
         raw1[0, 1] = load_weight(w1, 0, 1, "raw101")
         raw1[1, 1] = load_weight(w1, 1, 1, "raw111")
-        load_planes(w4s, w4_scales, nc.sync)
+        raw3[0] = load_weight(w3, 0, 0, "raw30")
         raw3[1] = load_weight(w3, 0, 1, "raw31")
         p1 = load_list(pos1, "p1")
-        p3 = load_list(pos3, "p3")
         raw5[0] = load_weight(w5, 0, 0, "raw50")
         raw5[1] = load_weight(w5, 1, 0, "raw51")
+        p3 = load_list(pos3, "p3")
+        load_planes(w4s, w4_scales, nc.sync)
         w4w = sb.tile([P, 2, N], U32, name="w4w", align_bytes=64)
         nc.sync.dma_start(w4w[:].bitcast(I32), w4_words.rearrange("g p c i -> p g (c i)").bitcast(I32))
         b5 = sb.tile([P, N // P], F32, name="b5")
@@ -137,8 +137,8 @@ def tile_list_pump_inspection_join_kernel(
             nc.vector.quantize_mx(out=codes[:].bitcast(FP8X4), scales=plane[:], in_=rounded[:])
             return codes, plane
 
-        def project(passes, bias):
-            win = sb.tile([P, S], F32, name="win", tag="win", bufs=16)
+        def project(passes, bias, tag, bufs):
+            win = sb.tile([P, S], F32, name=tag, tag=tag, bufs=bufs)
             for h in range(S // BANK):
                 cols = slice(h * BANK, (h + 1) * BANK)
                 bank = psum.tile([P, BANK], F32, name="bank", tag="bank")
@@ -159,7 +159,7 @@ def tile_list_pump_inspection_join_kernel(
                 c0 = g * PASS + t * P
                 win = project(
                     [(w2wp[:, 2 * c0 : 2 * (c0 + P)].bitcast(FP4X4), w2sp[:, c0 : c0 + P], g2w, g2s)],
-                    b2[:, PACK * g + t : PACK * g + t + 1],
+                    b2[:, PACK * g + t : PACK * g + t + 1], "bdwin", 8,
                 )
                 pick = sb.tile([P, J], F32, name="pick", tag="pick", bufs=8)
                 nc.vector.tensor_copy(pick[:], win[:].indirect(p2[:]))
@@ -175,7 +175,7 @@ def tile_list_pump_inspection_join_kernel(
                         (q1[a, g][0][:, cols].bitcast(FP8X4), q1[a, g][1][:, cols], g1w[a], g1s[4 * a :, :])
                         for a in range(2)
                     ],
-                    None,
+                    None, "awin", 4,
                 )
                 ab = sb.tile([P, J], F32, name="prod", tag="prod", bufs=8)
                 nc.vector.tensor_tensor(ab[:], win[:].indirect(p1[:]), picks[t][:], ALU.mult)
@@ -186,7 +186,7 @@ def tile_list_pump_inspection_join_kernel(
             wins = []
             for t in range(PACK):
                 cols = slice(t * P, (t + 1) * P)
-                wins.append(project([(q3[g][0][:, cols].bitcast(FP8X4), q3[g][1][:, cols], g3w, g3s)], None))
+                wins.append(project([(q3[g][0][:, cols].bitcast(FP8X4), q3[g][1][:, cols], g3w, g3s)], None, "bdwin", 8))
             return wins
 
         def join(z, wins, prods, j0, width):
@@ -210,9 +210,9 @@ def tile_list_pump_inspection_join_kernel(
         )
         q1[0, 0] = quantise(deal(raw1[0, 0]), "q100")
         q1[1, 0] = quantise(deal(raw1[1, 0]), "q110")
-        q3[0] = quantise(deal(raw3[0]), "q30")
         q1[0, 1] = quantise(deal(raw1[0, 1]), "q101")
         q1[1, 1] = quantise(deal(raw1[1, 1]), "q111")
+        q3[0] = quantise(deal(raw3[0]), "q30")
         q3[1] = quantise(deal(raw3[1]), "q31")
         g1s = gather(s1, l1, U8, "g1s")
         g1w[0] = gather(t1[0], l1, U32, "g1w0")
@@ -258,10 +258,10 @@ def tile_list_pump_inspection_join_kernel(
             parts = 2 if s == len(SLICES) - 1 else 1
             group = per_bank // parts
             for b in range(nbanks):
-                size = sb.tile([P, BANK], F32, name="pick", tag="pick", bufs=8)
-                root = sb.tile([P, BANK], F32, name="pick", tag="pick", bufs=8)
-                half = sb.tile([P, BANK], F32, name="pick", tag="pick", bufs=8)
-                res = sb.tile([P, BANK], F32, name="pick", tag="pick", bufs=8)
+                root = sb.tile([P, BANK], F32, name="root", tag="pick", bufs=8)
+                size = root
+                res = sb.tile([P, BANK], F32, name="res", tag="pick", bufs=8)
+                half = res
                 for part in range(parts):
                     c0 = b * per_bank + part * group
                     span = slice(part * group * width, (part + 1) * group * width)

@@ -93,13 +93,13 @@ def tile_list_pump_inspection_join_kernel(
         t1[1] = load_words(tab_words[1], "t11")
         t3 = load_words(tab3_words[0], "t3")
         p2 = load_list(pos2, "p2")
+        raw5[0] = load_weight(w5, 0, 0, "raw50")
         raw1[0, 1] = load_weight(w1, 0, 1, "raw101")
+        raw5[1] = load_weight(w5, 1, 0, "raw51")
         raw1[1, 1] = load_weight(w1, 1, 1, "raw111")
         raw3[0] = load_weight(w3, 0, 0, "raw30")
         raw3[1] = load_weight(w3, 0, 1, "raw31")
         p1 = load_list(pos1, "p1")
-        raw5[0] = load_weight(w5, 0, 0, "raw50")
-        raw5[1] = load_weight(w5, 1, 0, "raw51")
         p3 = load_list(pos3, "p3")
         load_planes(w4s, w4_scales, nc.sync)
         w4w = sb.tile([P, 2, N], U32, name="w4w", align_bytes=64)
@@ -128,6 +128,16 @@ def tile_list_pump_inspection_join_kernel(
                 t[:].rearrange("p (c i j) -> p c j i", i=4, j=PACK),
                 raw.rearrange("p j (c i) -> p c j i", i=4),
             )
+            return t
+
+        def weave_on_gpsimd(raw):
+            t = sb.tile([P, PACK * PASS], BF16, name="rounded5", tag="rounded5", bufs=2, align_bytes=64)
+            step = PASS // 2
+            for c0 in range(0, PASS, step):
+                nc.gpsimd.tensor_scalar(
+                    t[:, PACK * c0 : PACK * (c0 + step)].rearrange("p (c j) -> p c j", j=PACK),
+                    raw[:, :, c0 : c0 + step].rearrange("p j c -> p c j"), 1.0, 0.0, ALU.mult, ALU.add,
+                )
             return t
 
         def quantise(rounded, name):
@@ -221,8 +231,8 @@ def tile_list_pump_inspection_join_kernel(
         g3w = gather(t3, l3, U32, "g3w")
         picks0 = fuel(0)
         picks1 = fuel(1)
-        q5[0] = quantise(weave(raw5[0][:], "rounded", RB, nc.scalar.copy), "q50")
-        q5[1] = quantise(weave(raw5[1][:], "rounded", RB, nc.vector.tensor_copy), "q51")
+        q5[0] = quantise(weave_on_gpsimd(raw5[0]), "q50")
+        q5[1] = quantise(weave_on_gpsimd(raw5[1]), "q51")
         prods0 = pumps(0, picks0)
         wins0 = cans(0)
         z0 = sb.tile([P, PACK, J], F32, name="z0", tag="z0")

from contextlib import ExitStack

import concourse.mybir as mybir

K, M, H, N, T, S, J = 1024, 512, 1024, 512, 2048, 1024, 512
FLOPS = 2 * (K * H * S + 2 * M * H * S + 2 * H * N * J)

F32 = mybir.dt.float32
BF16 = mybir.dt.bfloat16
I32 = mybir.dt.int32
U32 = mybir.dt.uint32
U16 = mybir.dt.uint16
U8 = mybir.dt.uint8
FP8X4 = mybir.dt.float8_e4m3fn_x4
FP4X4 = mybir.dt.float4_e2m1fn_x4
ACT = mybir.ActivationFunctionType
ALU = mybir.AluOpType

P = 128
PACK = 4
PASS = P * PACK
BANK = 512
SLICES = (128, 128, 128, 128)
RB = 4


def tile_list_pump_inspection_join_kernel(
    tc, tab_words, tab_scales, tab2_words, tab2_scales, tab3_words, tab3_scales, offs, offs2, offs3,
    pos1, pos2, pos3, w1, w2_words, w2_scales, bias2, w3, w4_words, w4_scales, w5, bias5, out,
):
    nc = tc.nc
    with ExitStack() as ctx:
        lists = ctx.enter_context(tc.tile_pool(name="lists", bufs=1))
        sb = ctx.enter_context(tc.tile_pool(name="sb", bufs=1))
        psum = ctx.enter_context(tc.psum_pool(name="psum", bufs=8))

        def load_list(src, name):
            t = lists.tile(list(src.shape), U16, name=name)
            nc.sync.dma_start(t[:], src)
            return t

        def plane_tile(width, name, *engines):
            t = sb.tile([P, width], U8, name=name, align_bytes=64)
            share = width // len(engines)
            for n, engine in enumerate(engines):
                engine.memset(t[:, n * share : (n + 1) * share].bitcast(I32), 0)
            return t

        def load_planes(t, scales, queue):
            rows = 4 * scales.shape[0]
            for q in range(4):
                if rows == 4:
                    queue.dma_start(t[q:P:32, :].bitcast(I32), scales[0, q:16:4, :].bitcast(I32))
                else:
                    queue.dma_start(
                        t[32 * q : 32 * q + rows, :].bitcast(I32), scales[:, 4 * q : 4 * q + 4, :].bitcast(I32)
                    )

        def load_words(words, name):
            t = sb.tile([P, T], U32, name=name, tag="big", bufs=6, align_bytes=64)
            nc.sync.dma_start(t[:].bitcast(I32), words.rearrange("p t i -> p (t i)").bitcast(I32))
            return t

        def load_weight(w, a, g, name):
            t = sb.tile([P, PACK, PASS], F32, name=name, tag="big", bufs=6, align_bytes=64)
            src = w[a * PASS : (a + 1) * PASS, g * PASS : (g + 1) * PASS]
            nc.sync.dma_start(t[:], src.rearrange("(p j) c -> p j c", j=PACK))
            return t

        s2 = plane_tile(T, "s2", nc.gpsimd, nc.vector)
        s1 = plane_tile(T, "s1", nc.vector)
        w2s = plane_tile(H, "w2s", nc.gpsimd)
        s3 = plane_tile(T, "s3", nc.gpsimd)
        w4s = plane_tile(N, "w4s", nc.gpsimd)
        raw1, raw3, raw5, t1 = {}, {}, {}, {}
        l2 = load_list(offs2, "l2")
        load_planes(s2, tab2_scales, nc.sync)
        w2w = sb.tile([P, 2 * H], U8, name="w2w", align_bytes=64)
        nc.sync.dma_start(w2w[:].bitcast(I32), w2_words[0].bitcast(I32))
        l1 = load_list(offs, "l1")
        t2 = load_words(tab2_words[0], "t2")
        l3 = load_list(offs3, "l3")
        load_planes(s1, tab_scales, nc.sync)
        raw1[0, 0] = load_weight(w1, 0, 0, "raw100")
        load_planes(w2s, w2_scales, nc.sync)
        raw1[1, 0] = load_weight(w1, 1, 0, "raw110")
        b2 = sb.tile([P, 2 * PACK], F32, name="b2")
        nc.sync.dma_start(
            b2[:].rearrange("p (g t) -> p g t", t=PACK), bias2.rearrange("(g p t) -> p g t", p=P, t=PACK)
        )
        load_planes(s3, tab3_scales, nc.sync)
        t1[0] = load_words(tab_words[0], "t10")
        t1[1] = load_words(tab_words[1], "t11")
        t3 = load_words(tab3_words[0], "t3")
        p2 = load_list(pos2, "p2")
        raw5[0] = load_weight(w5, 0, 0, "raw50")
        raw1[0, 1] = load_weight(w1, 0, 1, "raw101")
        raw5[1] = load_weight(w5, 1, 0, "raw51")
        raw1[1, 1] = load_weight(w1, 1, 1, "raw111")
        raw3[0] = load_weight(w3, 0, 0, "raw30")
        raw3[1] = load_weight(w3, 0, 1, "raw31")
        p1 = load_list(pos1, "p1")
        p3 = load_list(pos3, "p3")
        load_planes(w4s, w4_scales, nc.sync)
        w4w = sb.tile([P, 2, N], U32, name="w4w", align_bytes=64)
        nc.sync.dma_start(w4w[:].bitcast(I32), w4_words.rearrange("g p c i -> p g (c i)").bitcast(I32))
        b5 = sb.tile([P, N // P], F32, name="b5")
        with nc.allow_non_contiguous_dma(reason="one bias value to a partition"):
            nc.sync.dma_start(b5[:], bias5.rearrange("(c p) -> p c", p=P))

        def gather(window, offsets, dtype, name):
            t = sb.tile([P, S], dtype, name=name, align_bytes=64)
            nc.vector.tensor_copy(t[:], window[:].indirect(offsets[:]))
            return t

        def deal(raw):
            t = sb.tile([P, PACK * PASS], BF16, name="rounded", tag="rounded", bufs=RB, align_bytes=64)
            nc.scalar.copy(
                t[:].rearrange("p (t m u e) -> p m u t e", t=PACK, u=2, e=2),
                raw[:].rearrange("p (u e) (m t) -> p m u t e", e=2, t=PACK),
            )
            return t

        def weave(raw, tag, bufs, copy):
            width = raw.shape[2]
            t = sb.tile([P, PACK * width], BF16, name=tag, tag=tag, bufs=bufs, align_bytes=64)
            copy(
                t[:].rearrange("p (c i j) -> p c j i", i=4, j=PACK),
                raw.rearrange("p j (c i) -> p c j i", i=4),
            )
            return t

        def weave_on_gpsimd(raw):
            t = sb.tile([P, PACK * PASS], BF16, name="rounded5", tag="rounded5", bufs=2, align_bytes=64)
            step = PASS // 2
            for c0 in range(0, PASS, step):
                nc.gpsimd.tensor_scalar(
                    t[:, PACK * c0 : PACK * (c0 + step)].rearrange("p (c j) -> p c j", j=PACK),
                    raw[:, :, c0 : c0 + step].rearrange("p j c -> p c j"), 1.0, 0.0, ALU.mult, ALU.add,
                )
            return t

        def quantise(rounded, name):
            width = rounded.shape[1] // PACK
            codes = sb.tile([P, width], U32, name=name + "c", align_bytes=64)
            plane = sb.tile([P, width], U8, name=name + "s", align_bytes=64)
            nc.vector.quantize_mx(out=codes[:].bitcast(FP8X4), scales=plane[:], in_=rounded[:])
            return codes, plane

        def project(passes, bias, tag, bufs):
            win = sb.tile([P, S], F32, name=tag, tag=tag, bufs=bufs)
            for h in range(S // BANK):
                cols = slice(h * BANK, (h + 1) * BANK)
                bank = psum.tile([P, BANK], F32, name="bank", tag="bank")
                for a, (wc, ws, vc, vs) in enumerate(passes):
                    nc.tensor.matmul_mx(
                        out=bank[:], lhsT=wc, lhsT_scale=ws, rhs=vc[:, cols].bitcast(FP8X4), rhs_scale=vs[:, cols],
                        start=(a == 0), stop=(a == len(passes) - 1),
                    )
                if bias is None:
                    nc.scalar.copy(win[:, cols], bank[:])
                else:
                    nc.scalar.activation(win[:, cols], bank[:], ACT.Identity, bias=bias)
            return win

        def fuel(g):
            picks = []
            for t in range(PACK):
                c0 = g * PASS + t * P
                win = project(
                    [(w2wp[:, 2 * c0 : 2 * (c0 + P)].bitcast(FP4X4), w2sp[:, c0 : c0 + P], g2w, g2s)],
                    b2[:, PACK * g + t : PACK * g + t + 1], "bdwin", 8,
                )
                pick = sb.tile([P, J], F32, name="pick", tag="pick", bufs=8)
                nc.vector.tensor_copy(pick[:], win[:].indirect(p2[:]))
                picks.append(pick)
            return picks

        def pumps(g, picks):
            prods = []
            for t in range(PACK):
                cols = slice(t * P, (t + 1) * P)
                win = project(
                    [
                        (q1[a, g][0][:, cols].bitcast(FP8X4), q1[a, g][1][:, cols], g1w[a], g1s[4 * a :, :])
                        for a in range(2)
                    ],
                    None, "awin", 4,
                )
                ab = sb.tile([P, J], F32, name="prod", tag="prod", bufs=8)
                nc.vector.tensor_tensor(ab[:], win[:].indirect(p1[:]), picks[t][:], ALU.mult)
                prods.append(ab)
            return prods

        def cans(g):
            wins = []
            for t in range(PACK):
                cols = slice(t * P, (t + 1) * P)
                wins.append(project([(q3[g][0][:, cols].bitcast(FP8X4), q3[g][1][:, cols], g3w, g3s)], None, "bdwin", 8))
            return wins

        def join(z, wins, prods, j0, width):
            for t in range(PACK):
                nc.vector.tensor_tensor(
                    z[:, t, :], wins[t][:].indirect(p3[:, j0 // 16 : (j0 + width) // 16]),
                    prods[t][:, j0 : j0 + width], ALU.add,
                )

        q1, q3, q5, g1w = {}, {}, {}, {}
        g2s = gather(s2, l2, U8, "g2s")
        w2wp = sb.tile([P, 2 * H], U8, name="w2wp", align_bytes=64)
        nc.scalar.copy(
            w2wp[:].bitcast(U16).rearrange("p (g t m) -> p g t m", g=2, t=PACK),
            w2w[:].bitcast(U16).rearrange("p (g m t) -> p g t m", g=2, t=PACK),
        )
        g2w = gather(t2, l2, U32, "g2w")
        w2sp = sb.tile([P, H], U8, name="w2sp", align_bytes=64)
        nc.vector.tensor_copy(
            w2sp[:].rearrange("p (g t m) -> p g t m", g=2, t=PACK), w2s[:].rearrange("p (g m t) -> p g t m", g=2, t=PACK)
        )
        q1[0, 0] = quantise(deal(raw1[0, 0]), "q100")
        q1[1, 0] = quantise(deal(raw1[1, 0]), "q110")
        q1[0, 1] = quantise(deal(raw1[0, 1]), "q101")
        q1[1, 1] = quantise(deal(raw1[1, 1]), "q111")
        q3[0] = quantise(deal(raw3[0]), "q30")
        q3[1] = quantise(deal(raw3[1]), "q31")
        g1s = gather(s1, l1, U8, "g1s")
        g1w[0] = gather(t1[0], l1, U32, "g1w0")
        g1w[1] = gather(t1[1], l1, U32, "g1w1")
        g3s = gather(s3, l3, U8, "g3s")
        g3w = gather(t3, l3, U32, "g3w")
        picks0 = fuel(0)
        picks1 = fuel(1)
        q5[0] = quantise(weave_on_gpsimd(raw5[0]), "q50")
        q5[1] = quantise(weave_on_gpsimd(raw5[1]), "q51")
        prods0 = pumps(0, picks0)
        wins0 = cans(0)
        z0 = sb.tile([P, PACK, J], F32, name="z0", tag="z0")
        join(z0, wins0, prods0, 0, J)
        prods1 = pumps(1, picks1)
        zq0 = quantise(weave(z0[:], "rounded", RB, nc.scalar.copy), "zq0")
        wins1 = cans(1)

        j0 = 0
        for s, width in enumerate(SLICES):
            jcols = slice(j0, j0 + width)
            per_bank = BANK // width
            nbanks = (N // P) // per_bank
            ztile = sb.tile([P, PACK, width], F32, name="z1", tag="z1", bufs=2)
            z = ztile[:]
            join(z, wins1, prods1, j0, width)
            zq1 = quantise(weave(z, "zround", 2, nc.vector.tensor_copy if "ssvv"[s] == "v" else nc.scalar.copy), "zq1%d" % s)
            y1 = [psum.tile([P, BANK], F32, name="bank", tag="bank") for b in range(nbanks)]
            y2 = [psum.tile([P, BANK], F32, name="bank", tag="bank") for b in range(nbanks)]
            for g, (zc, zs) in enumerate(((zq0[0][:, jcols], zq0[1][:, jcols]), (zq1[0][:], zq1[1][:]))):
                for banks, wc, ws in (
                    (y2, q5[g][0][:], q5[g][1][:]),
                    (y1, w4w[:, g, :], w4s[4 * g :, :]),
                ):
                    for c in range(N // P):
                        place = c % per_bank
                        nc.tensor.matmul_mx(
                            out=banks[c // per_bank][:, place * width : (place + 1) * width],
                            lhsT=wc[:, c * P : (c + 1) * P].bitcast(FP8X4), lhsT_scale=ws[:, c * P : (c + 1) * P],
                            rhs=zc.bitcast(FP8X4), rhs_scale=zs,
                            start=(g == 0 and place == 0), stop=(g == 1 and place == per_bank - 1),
                        )
            parts = 2 if s == len(SLICES) - 1 else 1
            group = per_bank // parts
            for b in range(nbanks):
                root = sb.tile([P, BANK], F32, name="root", tag="pick", bufs=8)
                size = root
                res = sb.tile([P, BANK], F32, name="res", tag="pick", bufs=8)
                half = res
                for part in range(parts):
                    c0 = b * per_bank + part * group
                    span = slice(part * group * width, (part + 1) * group * width)
                    for c in range(c0, c0 + group):
                        cols = slice((c % per_bank) * width, (c % per_bank + 1) * width)
                        nc.scalar.activation(size[:, cols], y2[b][:, cols], ACT.Abs, bias=b5[:, c : c + 1])
                    nc.scalar.activation(root[:, span], size[:, span], ACT.Abs_reciprocal_sqrt, bias=1.0)
                    if "vvvv"[s] == "s":
                        nc.scalar.activation(half[:, span], root[:, span], ACT.Square)
                        nc.vector.tensor_tensor(res[:, span], y1[b][:, span], half[:, span], ALU.mult)
                    else:
                        nc.vector.tensor_tensor(half[:, span], y1[b][:, span], root[:, span], ALU.mult)
                        nc.vector.tensor_tensor(res[:, span], half[:, span], root[:, span], ALU.mult)
                    rows = out[c0 * P : (c0 + group) * P, jcols]
                    nc.sync.dma_start(
                        rows.rearrange("(c p) j -> p c j", p=P), res[:, span].rearrange("p (c j) -> p c j", j=width)
                    )
            j0 = j0 + width
